import numpy as np
import ml_dtypes


def mxq(x, axis, fmt="e4m3"):
    dtype, down = {"e4m3": (ml_dtypes.float8_e4m3fn, 7), "e5m2": (ml_dtypes.float8_e5m2, 14)}[fmt]
    v = np.moveaxis(np.asarray(x, np.float32).astype(ml_dtypes.bfloat16).astype(np.float64), axis, -1)
    blocks = v.reshape(v.shape[:-1] + (-1, 32))
    amax = np.abs(blocks).max(-1, keepdims=True)
    byte = np.maximum(np.where(amax > 0, np.frexp(amax)[1] - 1 + 127, 0) - down, 1)
    scale = np.exp2(byte - 127.0)
    codes = (blocks / scale).astype(np.float32).astype(dtype).astype(np.float64)
    return np.moveaxis((codes * scale).reshape(v.shape), -1, axis)


WIDE = False


def mx_kscale(k):
    if not WIDE:
        return np.ones(k)
    levels = np.array([10, -10, 5, -5, 0])
    if k % 512:
        return np.exp2(np.random.permutation(np.resize(levels, k // 32))).repeat(32)
    a = np.empty((k // 512, 16))
    for p in range(k // 512):
        a[p, :8] = np.random.permutation(np.resize(levels, 8))
        for g in range(8):
            far = levels[np.abs(levels - a[p, g]) >= 10]
            a[p, g + 8] = far[np.random.randint(len(far))]
    return np.exp2(a.ravel()).repeat(32)


def f64(x):
    return np.asarray(x).astype(np.float64)


def striped(idx):
    return np.tile(idx.reshape(-1, 16).T, (8, 1)).astype(np.uint16)


def unstriped(offs):
    return offs[:16].T.reshape(-1).astype(np.int64)


def striped8(idx):
    return np.concatenate([x.reshape(-1, 16).T for x in idx]).astype(np.uint16)


def runs(offs, k):
    lists = np.stack([offs[16 * r : 16 * r + 16].T.reshape(-1) for r in range(8)]).astype(np.int64)
    return lists[np.arange(k) % 512 // 64]


def pack_weight(w):
    k, n = w.shape
    w = f64(np.asarray(w, np.float32).astype(ml_dtypes.bfloat16)).reshape(k // 32, 32, n)
    amax = np.abs(w).max(1)
    byte = np.clip(np.where(amax > 0, np.frexp(amax)[1] - 1 + 127 - 7, 1), 1, 254)
    scaled = (w * np.exp2(127.0 - byte)[:, None, :]).reshape(k, n).astype(np.float32)
    words = np.ascontiguousarray(scaled.reshape(k // 512, 128, 4, n).transpose(0, 1, 3, 2)).astype(ml_dtypes.float8_e4m3fn).view(np.uint8)
    return words, np.ascontiguousarray(byte.astype(np.uint8).reshape(k // 512, 16, n))


def unpack_weight(words, scales):
    g, p, n, _ = words.shape
    vals = np.ascontiguousarray(words).view(ml_dtypes.float8_e4m3fn).astype(np.float64) * np.repeat(np.exp2(scales.astype(np.float64) - 127.0), 8, axis=1)[..., None]
    return vals.transpose(0, 1, 3, 2).reshape(g * 512, n)

def planes(y):
    n, m = y.shape
    v = y.astype(np.float32).astype(ml_dtypes.bfloat16).astype(np.float64).reshape(n // 32, 32, m)
    top = np.abs(v).max(1)
    byte = np.clip(np.where(top > 0, np.frexp(top)[1] - 1 + 127 - 7, 1), 1, 254)
    codes = (v * np.exp2(127.0 - byte)[:, None, :]).reshape(n, m).astype(np.float32).astype(ml_dtypes.float8_e4m3fn).view(np.uint8)
    words = codes.reshape(n // 512, 128, 4, m).transpose(0, 1, 3, 2)
    return np.ascontiguousarray(words), np.ascontiguousarray(byte.astype(np.uint8).reshape(n // 512, 16, m))


K, T, S, N, H, W = 512, 2048, 512, 512, 512, 384


def setup_inputs():
    n = np.random.standard_normal
    s = mx_kscale(K)[:, None]
    u = mx_kscale(H)
    packed_xT = pack_weight(n((K, T)) * s)
    packed_w1 = pack_weight(n((K, H)) / np.sqrt(K) / s)
    packed_w2 = pack_weight(n((H, N)) / np.sqrt(H) / u[:, None])
    return {
        "x_words": packed_xT[0],
        "x_scales": packed_xT[1],
        "w1_words": packed_w1[0],
        "w1_scales": packed_w1[1],
        "gn": (np.random.uniform(0.5, 1.5, (H, 1)) * u[:, None]).astype(np.float32),
        "w2_words": packed_w2[0],
        "w2_scales": packed_w2[1],
        "offs": striped8(np.random.randint(0, T, (8, S))),
        "n1": striped(np.random.permutation(S)),
        "n2": striped(np.random.permutation(S)),
        "n3": striped(np.random.permutation(S)[:W]),
        "n4": striped(np.random.permutation(S)[:W]),
    }


def reference(x_words, x_scales, w1_words, w1_scales, gn, w2_words, w2_scales, offs, n1, n2, n3, n4):
    xq = unpack_weight(x_words, x_scales)[np.arange(K)[:, None], runs(offs, K)]
    y = unpack_weight(w1_words, w1_scales).T @ xq
    st = y - y[:, unstriped(n1)]
    z = f64(gn) * (st / (np.abs(st[:, unstriped(n2)]) + 0.5))
    h = unpack_weight(w2_words, w2_scales).T @ mxq(z, 0, "e4m3")
    old = h[:, unstriped(n3)]
    pa = h[:, unstriped(n4)]
    ra = old - (0.5 * pa)
    out = h.copy()
    out[:, unstriped(n3)] = ra
    return (out,) + planes(out)

@@ -1,0 +1,270 @@
+import concourse.mybir as mybir
+
+K, T, S, N, H, W = 512, 2048, 512, 512, 512, 384
+FLOPS = 2 * K * H * S + 2 * H * N * S
+
+F32 = mybir.dt.float32
+BF16 = mybir.dt.bfloat16
+I32 = mybir.dt.int32
+U32 = mybir.dt.uint32
+U16 = mybir.dt.uint16
+U8 = mybir.dt.uint8
+FP8X4 = mybir.dt.float8_e4m3fn_x4
+ALU = mybir.AluOpType
+ACT = mybir.ActivationFunctionType
+
+P = 128
+PACK = 4
+SPARE = 16
+ALL = slice(0, S)
+HALVES = [(slice(0, S // 2), slice(0, S // 32)), (slice(S // 2, S), slice(S // 32, S // 16))]
+(FIRST, FIRST_ENTRIES), (SECOND, SECOND_ENTRIES) = HALVES
+
+
+def words_view(dram_words):
+    return dram_words[0].rearrange("p n t -> p (n t)").bitcast(I32)
+
+
+def load_scale_rows(queues, plane, dram_scales):
+    rows = dram_scales[0].bitcast(I32)
+    for q in range(4):
+        queues[q].dma_start(plane[32 * q : 32 * q + 4, :].bitcast(I32), rows[4 * q : 4 * q + 4, :])
+
+
+def deal(engine, dealt, raw):
+    engine.tensor_copy(dealt.rearrange("p (t m) -> p t m", t=PACK), raw.rearrange("p (m t) -> p t m", t=PACK))
+
+
+def tile_picked_hashhopnkdif_none_po_kernel(
+    tc, x_words, x_scales, w1_words, w1_scales, gn, w2_words, w2_scales, offs, n1, n2, n3, n4, out_0, out_1, out_2
+):
+    nc = tc.nc
+    with tc.tile_pool(name="keep", bufs=1) as keep, tc.psum_pool(name="psum", bufs=1) as psum:
+
+        def sbuf(name, shape, dtype, tag=None):
+            return keep.tile(shape, dtype, name=name, tag=tag or name, align_bytes=64)
+
+        offs_t = sbuf("offs_t", [P, S // 16], U16)
+        n1_t = sbuf("n1_t", [P, S // 16], U16)
+        n2_t = sbuf("n2_t", [P, S // 16], U16)
+        n3_t = sbuf("n3_t", [P, W // 16], U16)
+        n4_t = sbuf("n4_t", [P, W // 16], U16)
+        x_tab = sbuf("x_tab", [P, T], U32)
+        xs_tab = sbuf("xs_tab", [P, T], U8)
+        xs_pick = sbuf("xs_pick", [P, S], U8)
+        xs_plane = sbuf("xs_plane", [P, S], U8)
+        w1_raw = sbuf("w1_raw", [P, H], U32)
+        w1s_raw = sbuf("w1s_raw", [P, H], U8)
+        w1_deal = sbuf("w1_deal", [P, H], U32)
+        w1s_deal = sbuf("w1s_deal", [P, H], U8)
+        w2_deal = sbuf("w2_deal", [P, N], U32)
+        w2s_deal = sbuf("w2s_deal", [P, N], U8)
+        gain = sbuf("gain", [P, PACK], F32)
+        half = sbuf("half", [P, 1], F32)
+        y_win = [sbuf("y_win%d" % t, [P, S + SPARE], F32) for t in range(PACK)]
+        r_win = [sbuf("r_win%d" % t, [P, S + SPARE], F32) for t in range(PACK)]
+
+        nc.gpsimd.memset(xs_tab[:].bitcast(I32), 0)
+        nc.gpsimd.memset(w1s_raw[:].bitcast(I32), 0)
+        nc.vector.memset(xs_plane[:].bitcast(I32), 0)
+        nc.vector.memset(half[:], 0.5)
+        for t in range(PACK):
+            nc.vector.memset(y_win[t][:, S:], 0.0)
+            nc.vector.memset(r_win[t][:, S:], 0.0)
+
+        nc.sync.dma_start(offs_t[:], offs)
+        nc.scalar.dma_start(xs_tab[0:P:8, :].bitcast(I32), x_scales[0].bitcast(I32))
+        load_scale_rows([nc.gpsimd, nc.gpsimd, nc.scalar, nc.scalar], w1s_raw, w1_scales)
+        nc.sync.dma_start(n1_t[:], n1)
+        nc.sync.dma_start(n2_t[:], n2)
+        nc.sync.dma_start(n3_t[:], n3)
+        nc.sync.dma_start(w1_raw[:].bitcast(I32), words_view(w1_words))
+        nc.sync.dma_start(x_tab[:].bitcast(I32), words_view(x_words))
+        nc.sync.dma_start(n4_t[:], n4)
+        nc.gpsimd.dma_start(gain[:], gn.rearrange("(p t) o -> p (t o)", t=PACK))
+
+        nc.vector.tensor_copy(xs_pick[:], xs_tab[:].indirect(offs_t[:]))
+        for j in range(4):
+            nc.scalar.dma_start(xs_plane[j:P:32, :].bitcast(I32), xs_pick[8 * j : P : 32, :].bitcast(I32))
+        deal(nc.vector, w1_deal[:], w1_raw[:])
+        deal(nc.gpsimd, w1s_deal[:], w1s_raw[:])
+        x_pick = sbuf("x_pick", [P, S], U32, tag="xs_tab")
+        for cols, entries in HALVES:
+            nc.vector.tensor_copy(x_pick[:, cols], x_tab[:].indirect(offs_t[:, entries]))
+
+        w2_raw = sbuf("w2_raw", [P, N], U32, tag="x_tab")
+        w2s_raw = sbuf("w2s_raw", [P, N], U8, tag="xs_pick")
+        nc.gpsimd.memset(w2s_raw[:].bitcast(I32), 0)
+        nc.sync.dma_start(w2_raw[:].bitcast(I32), words_view(w2_words))
+        load_scale_rows([nc.sync] * 4, w2s_raw, w2_scales)
+        deal(nc.gpsimd, w2_deal[:], w2_raw[:])
+        deal(nc.gpsimd, w2s_deal[:], w2s_raw[:])
+
+        def product(name, t, cols, w_deal, ws_deal, codes, scales):
+            acc = psum.tile([P, cols.stop - cols.start], F32, name=name, tag="bank_%d_%d" % (t, cols.start))
+            rows = slice(t * P, (t + 1) * P)
+            nc.tensor.matmul_mx(
+                out=acc[:],
+                lhsT=w_deal[:, rows].bitcast(FP8X4),
+                lhsT_scale=ws_deal[:, rows],
+                rhs=codes[:, cols].bitcast(FP8X4),
+                rhs_scale=scales[:, cols],
+                start=True,
+                stop=True,
+            )
+            return acc
+
+        def products(name, w_deal, ws_deal, codes, scales):
+            parts = [[FIRST, SECOND], [ALL], [ALL], [ALL]]
+            return [
+                [(cols, product("%s%d_%d" % (name, t, cols.start), t, cols, w_deal, ws_deal, codes, scales)) for cols in parts[t]]
+                for t in range(PACK)
+            ]
+
+        y_n1 = [sbuf("y_n1_%d" % t, [P, S], F32) for t in range(PACK)]
+        st = [sbuf("st%d" % t, [P, S], F32) for t in range(PACK)]
+        size = [sbuf("size%d" % t, [P, S], F32) for t in range(PACK)]
+        root = [sbuf("root%d" % t, [P, S], F32) for t in range(PACK)]
+        r_n2 = [sbuf("r_n2_%d" % t, [P, S], F32) for t in range(PACK)]
+        z = sbuf("z", [P, PACK, S], F32)
+        z_bf = sbuf("z_bf", [P, S, PACK], BF16)
+        z_codes = sbuf("z_codes", [P, S], U32)
+        z_scales = sbuf("z_scales", [P, S], U8)
+
+        y_acc = products("y_acc", w1_deal, w1s_deal, x_pick, xs_plane)
+
+        def leave_banks(acc, win, t):
+            for cols, bank in acc[t]:
+                if cols is FIRST:
+                    nc.scalar.copy(win[:, cols], bank[:])
+                else:
+                    nc.vector.tensor_copy(win[:, cols], bank[:])
+
+        def fetch_n1(t):
+            for cols, bank in y_acc[t]:
+                entries = slice(cols.start // 16, cols.stop // 16)
+                nc.scalar.activation(y_n1[t][:, cols], y_win[t][:].indirect(n1_t[:, entries]), ACT.Copy)
+
+        def subtract(t):
+            for cols, bank in y_acc[t]:
+                nc.vector.tensor_tensor(st[t][:, cols], bank[:], y_n1[t][:, cols], ALU.subtract)
+
+        def size_on_vector(t):
+            nc.vector.scalar_tensor_tensor(size[t][:], st[t][:], -1.0, st[t][:], ALU.mult, ALU.max)
+
+        def size_on_scalar(t):
+            nc.scalar.activation(size[t][:], st[t][:], ACT.Abs)
+
+        def inverse_root(t):
+            nc.scalar.activation(root[t][:], size[t][:], ACT.Abs_reciprocal_sqrt, bias=half[:])
+
+        def ratio(t):
+            nc.vector.scalar_tensor_tensor(
+                r_win[t][:, :S], root[t][:], gain[:, t : t + 1], root[t][:], ALU.mult, ALU.mult
+            )
+
+        def fetch_n2_times_st(t, part):
+            cols, entries = HALVES[part]
+            nc.vector.tensor_tensor(z[:, t, cols], r_win[t][:].indirect(n2_t[:, entries]), st[t][:, cols], ALU.mult)
+
+        def fetch_n2(t, part):
+            cols, entries = HALVES[part]
+            nc.scalar.activation(r_n2[t][:, cols], r_win[t][:].indirect(n2_t[:, entries]), ACT.Copy)
+
+        def times_st(t, part):
+            cols, entries = HALVES[part]
+            nc.vector.tensor_tensor(z[:, t, cols], r_n2[t][:, cols], st[t][:, cols], ALU.mult)
+
+        def quantise(codes, scales, grouped, cols):
+            nc.vector.quantize_mx(
+                out=codes[:, cols].bitcast(FP8X4),
+                scales=scales[:, cols],
+                in_=grouped[:, cols, :].rearrange("p s t -> p (s t)"),
+            )
+
+        leave_banks(y_acc, y_win[0], 0)
+        fetch_n1(0)
+        leave_banks(y_acc, y_win[1], 1)
+        leave_banks(y_acc, y_win[2], 2)
+        fetch_n1(1)
+        subtract(0)
+        leave_banks(y_acc, y_win[3], 3)
+        size_on_vector(0)
+        fetch_n1(2)
+        subtract(1)
+        inverse_root(0)
+        size_on_vector(1)
+        subtract(2)
+        inverse_root(1)
+        ratio(0)
+        fetch_n1(3)
+        ratio(1)
+        fetch_n2_times_st(0, 0)
+        size_on_scalar(2)
+        subtract(3)
+        inverse_root(2)
+        fetch_n2_times_st(1, 0)
+        size_on_scalar(3)
+        ratio(2)
+        inverse_root(3)
+        fetch_n2_times_st(0, 1)
+        fetch_n2(2, 0)
+        ratio(3)
+        fetch_n2_times_st(1, 1)
+        fetch_n2(3, 0)
+        times_st(2, 0)
+        fetch_n2(3, 1)
+        times_st(3, 0)
+        fetch_n2_times_st(2, 1)
+        nc.scalar.copy(z_bf[:, FIRST, :], z[:, :, FIRST].rearrange("p t s -> p s t"))
+        times_st(3, 1)
+        nc.vector.tensor_copy(z_bf[:, SECOND, :], z[:, :, SECOND].rearrange("p t s -> p s t"))
+        quantise(z_codes, z_scales, z_bf, FIRST)
+        quantise(z_codes, z_scales, z_bf, SECOND)
+
+        o_bf = sbuf("o_bf", [P, S, PACK], BF16)
+        o_codes = sbuf("o_codes", [P, S], U32)
+        o_scales = sbuf("o_scales", [P, S], U8)
+        o_win = [sbuf("o_win%d" % t, [P, S], F32) for t in range(PACK)]
+        old2 = [sbuf("old2_%d" % t, [P, W], F32) for t in range(PACK)]
+        ra2 = [sbuf("ra2_%d" % t, [P, W], F32) for t in range(PACK)]
+        out_rows = out_0.rearrange("(p t) s -> p t s", t=PACK)
+        h_acc = products("h_acc", w2_deal, w2s_deal, z_codes, z_scales)
+
+        def fetch_n3(t):
+            nc.scalar.activation(old2[t][:], o_win[t][:].indirect(n3_t[:]), ACT.Copy, scale=-2.0)
+
+        def fetch_n4_plus(t):
+            nc.vector.tensor_tensor(ra2[t][:], o_win[t][:].indirect(n4_t[:]), old2[t][:], ALU.add)
+
+        def put_n3(t):
+            nc.scalar.activation(o_win[t][:].indirect(n3_t[:]), ra2[t][:], ACT.Copy, scale=-0.5)
+            nc.sync.dma_start(out_rows[:, t, :], o_win[t][:])
+
+        def round_plane(t, cols):
+            nc.vector.tensor_copy(o_bf[:, cols, t], o_win[t][:, cols])
+
+        for t in range(3):
+            leave_banks(h_acc, o_win[t], t)
+            fetch_n3(t)
+        fetch_n4_plus(0)
+        leave_banks(h_acc, o_win[3], 3)
+        put_n3(0)
+        fetch_n4_plus(1)
+        fetch_n3(3)
+        fetch_n4_plus(2)
+        round_plane(0, ALL)
+        fetch_n4_plus(3)
+        for t in range(1, 3):
+            put_n3(t)
+            round_plane(t, ALL)
+        put_n3(3)
+        round_plane(3, FIRST)
+        round_plane(3, SECOND)
+        code_words = words_view(out_1)
+        for cols in (FIRST, SECOND):
+            quantise(o_codes, o_scales, o_bf, cols)
+            nc.sync.dma_start(code_words[:, cols], o_codes[:, cols].bitcast(I32))
+        scale_rows = out_2[0].bitcast(I32)
+        for q in range(4):
+            nc.scalar.dma_start(scale_rows[4 * q : 4 * q + 4, :], o_scales[32 * q : 32 * q + 4, :].bitcast(I32))

@@ -64,33 +64,41 @@ def tile_picked_hashhopnkdif_none_po_kernel(
         y_win = [sbuf("y_win%d" % t, [P, S + SPARE], F32) for t in range(PACK)]
         r_win = [sbuf("r_win%d" % t, [P, S + SPARE], F32) for t in range(PACK)]
 
-        nc.gpsimd.memset(xs_tab[:].bitcast(I32), 0)
+        xs_words = xs_tab[:].bitcast(I32)
+        nc.vector.memset(xs_words[:, :384], 0)
+        nc.gpsimd.memset(xs_words[:, 384:], 0)
         nc.gpsimd.memset(w1s_raw[:].bitcast(I32), 0)
-        nc.vector.memset(xs_plane[:].bitcast(I32), 0)
-        nc.vector.memset(half[:], 0.5)
         for t in range(PACK):
             nc.vector.memset(y_win[t][:, S:], 0.0)
             nc.vector.memset(r_win[t][:, S:], 0.0)
+        nc.vector.memset(half[:], 0.5)
 
         nc.sync.dma_start(offs_t[:], offs)
-        nc.scalar.dma_start(xs_tab[0:P:8, :].bitcast(I32), x_scales[0].bitcast(I32))
-        load_scale_rows([nc.gpsimd, nc.gpsimd, nc.scalar, nc.scalar], w1s_raw, w1_scales)
+        xs_rows = x_scales[0].bitcast(I32)
+        for j in range(2):
+            nc.sync.dma_start(xs_tab[j:P:16, :].bitcast(I32), xs_rows[j:16:2, :])
+        load_scale_rows([nc.scalar] * 4, w1s_raw, w1_scales)
+        nc.sync.dma_start(x_tab[:].bitcast(I32), words_view(x_words))
+        nc.sync.dma_start(w1_raw[:].bitcast(I32), words_view(w1_words))
         nc.sync.dma_start(n1_t[:], n1)
         nc.sync.dma_start(n2_t[:], n2)
         nc.sync.dma_start(n3_t[:], n3)
-        nc.sync.dma_start(w1_raw[:].bitcast(I32), words_view(w1_words))
-        nc.sync.dma_start(x_tab[:].bitcast(I32), words_view(x_words))
         nc.sync.dma_start(n4_t[:], n4)
+        warm = sbuf("warm", [P, 1], F32)
+        nc.scalar.activation(warm[:], half[:], ACT.Abs_reciprocal_sqrt, bias=half[:])
         nc.gpsimd.dma_start(gain[:], gn.rearrange("(p t) o -> p (t o)", t=PACK))
 
         nc.vector.tensor_copy(xs_pick[:], xs_tab[:].indirect(offs_t[:]))
-        for j in range(4):
-            nc.scalar.dma_start(xs_plane[j:P:32, :].bitcast(I32), xs_pick[8 * j : P : 32, :].bitcast(I32))
-        deal(nc.vector, w1_deal[:], w1_raw[:])
+        nc.vector.tensor_copy(xs_plane[:].bitcast(I32), xs_pick[:].bitcast(I32))
+        for j in range(2):
+            nc.scalar.dma_start(xs_plane[2 + j : P : 32, :].bitcast(I32), xs_pick[16 + j : P : 32, :].bitcast(I32))
         deal(nc.gpsimd, w1s_deal[:], w1s_raw[:])
         x_pick = sbuf("x_pick", [P, S], U32, tag="xs_tab")
-        for cols, entries in HALVES:
-            nc.vector.tensor_copy(x_pick[:, cols], x_tab[:].indirect(offs_t[:, entries]))
+        nc.vector.tensor_copy(x_pick[:, FIRST], x_tab[:].indirect(offs_t[:, FIRST_ENTRIES]))
+        w1_by_tile = w1_raw[:].rearrange("p (m t) -> p t m", t=PACK)
+        nc.vector.tensor_copy(w1_deal[:, :P], w1_by_tile[:, 0, :])
+        nc.vector.tensor_copy(x_pick[:, SECOND], x_tab[:].indirect(offs_t[:, SECOND_ENTRIES]))
+        nc.gpsimd.tensor_copy(w1_deal[:, P:].rearrange("p (t m) -> p t m", m=P), w1_by_tile[:, 1:, :])
 
         w2_raw = sbuf("w2_raw", [P, N], U32, tag="x_tab")
         w2s_raw = sbuf("w2s_raw", [P, N], U8, tag="xs_pick")

@@ -65,9 +65,9 @@ def tile_picked_hashhopnkdif_none_po_kernel(
         r_win = [sbuf("r_win%d" % t, [P, S + SPARE], F32) for t in range(PACK)]
 
         xs_words = xs_tab[:].bitcast(I32)
-        nc.vector.memset(xs_words[:, :384], 0)
-        nc.gpsimd.memset(xs_words[:, 384:], 0)
-        nc.gpsimd.memset(w1s_raw[:].bitcast(I32), 0)
+        nc.vector.memset(w1s_raw[:].bitcast(I32), 0)
+        nc.vector.memset(xs_words[:, :192], 0)
+        nc.gpsimd.memset(xs_words[:, 192:], 0)
         for t in range(PACK):
             nc.vector.memset(y_win[t][:, S:], 0.0)
             nc.vector.memset(r_win[t][:, S:], 0.0)
@@ -76,8 +76,8 @@ def tile_picked_hashhopnkdif_none_po_kernel(
         nc.sync.dma_start(offs_t[:], offs)
         xs_rows = x_scales[0].bitcast(I32)
         for j in range(2):
-            nc.sync.dma_start(xs_tab[j:P:16, :].bitcast(I32), xs_rows[j:16:2, :])
-        load_scale_rows([nc.scalar] * 4, w1s_raw, w1_scales)
+            nc.scalar.dma_start(xs_tab[j:P:16, :].bitcast(I32), xs_rows[j:16:2, :])
+        load_scale_rows([nc.sync] * 4, w1s_raw, w1_scales)
         nc.sync.dma_start(x_tab[:].bitcast(I32), words_view(x_words))
         nc.sync.dma_start(w1_raw[:].bitcast(I32), words_view(w1_words))
         nc.sync.dma_start(n1_t[:], n1)

import concourse.mybir as mybir

K, T, S, N, H, W = 512, 2048, 512, 512, 512, 384
FLOPS = 2 * K * H * S + 2 * H * N * S

F32 = mybir.dt.float32
BF16 = mybir.dt.bfloat16
I32 = mybir.dt.int32
U32 = mybir.dt.uint32
U16 = mybir.dt.uint16
U8 = mybir.dt.uint8
FP8X4 = mybir.dt.float8_e4m3fn_x4
ALU = mybir.AluOpType
ACT = mybir.ActivationFunctionType

P = 128
PACK = 4
SPARE = 16
ALL = slice(0, S)
HALVES = [(slice(0, S // 2), slice(0, S // 32)), (slice(S // 2, S), slice(S // 32, S // 16))]
(FIRST, FIRST_ENTRIES), (SECOND, SECOND_ENTRIES) = HALVES


def words_view(dram_words):
    return dram_words[0].rearrange("p n t -> p (n t)").bitcast(I32)


def load_scale_rows(queues, plane, dram_scales):
    rows = dram_scales[0].bitcast(I32)
    for q in range(4):
        queues[q].dma_start(plane[32 * q : 32 * q + 4, :].bitcast(I32), rows[4 * q : 4 * q + 4, :])


def deal(engine, dealt, raw):
    engine.tensor_copy(dealt.rearrange("p (t m) -> p t m", t=PACK), raw.rearrange("p (m t) -> p t m", t=PACK))


def tile_picked_hashhopnkdif_none_po_kernel(
    tc, x_words, x_scales, w1_words, w1_scales, gn, w2_words, w2_scales, offs, n1, n2, n3, n4, out_0, out_1, out_2
):
    nc = tc.nc
    with tc.tile_pool(name="keep", bufs=1) as keep, tc.psum_pool(name="psum", bufs=1) as psum:

        def sbuf(name, shape, dtype, tag=None):
            return keep.tile(shape, dtype, name=name, tag=tag or name, align_bytes=64)

        offs_t = sbuf("offs_t", [P, S // 16], U16)
        n1_t = sbuf("n1_t", [P, S // 16], U16)
        n2_t = sbuf("n2_t", [P, S // 16], U16)
        n3_t = sbuf("n3_t", [P, W // 16], U16)
        n4_t = sbuf("n4_t", [P, W // 16], U16)
        x_tab = sbuf("x_tab", [P, T], U32)
        xs_tab = sbuf("xs_tab", [P, T], U8)
        xs_pick = sbuf("xs_pick", [P, S], U8)
        xs_plane = sbuf("xs_plane", [P, S], U8)
        w1_raw = sbuf("w1_raw", [P, H], U32)
        w1s_raw = sbuf("w1s_raw", [P, H], U8)
        w1_deal = sbuf("w1_deal", [P, H], U32)
        w1s_deal = sbuf("w1s_deal", [P, H], U8)
        w2_deal = sbuf("w2_deal", [P, N], U32)
        w2s_deal = sbuf("w2s_deal", [P, N], U8)
        gain = sbuf("gain", [P, PACK], F32)
        half = sbuf("half", [P, 1], F32)
        y_win = [sbuf("y_win%d" % t, [P, S + SPARE], F32) for t in range(PACK)]
        r_win = [sbuf("r_win%d" % t, [P, S + SPARE], F32) for t in range(PACK)]

        xs_words = xs_tab[:].bitcast(I32)
        nc.vector.memset(w1s_raw[:].bitcast(I32), 0)
        nc.vector.memset(xs_words[:, :192], 0)
        nc.gpsimd.memset(xs_words[:, 192:], 0)
        for t in range(PACK):
            nc.vector.memset(y_win[t][:, S:], 0.0)
            nc.vector.memset(r_win[t][:, S:], 0.0)
        nc.vector.memset(half[:], 0.5)

        nc.sync.dma_start(offs_t[:], offs)
        xs_rows = x_scales[0].bitcast(I32)
        for j in range(2):
            nc.scalar.dma_start(xs_tab[j:P:16, :].bitcast(I32), xs_rows[j:16:2, :])
        load_scale_rows([nc.sync] * 4, w1s_raw, w1_scales)
        nc.sync.dma_start(x_tab[:].bitcast(I32), words_view(x_words))
        nc.sync.dma_start(w1_raw[:].bitcast(I32), words_view(w1_words))
        nc.sync.dma_start(n1_t[:], n1)
        nc.sync.dma_start(n2_t[:], n2)
        nc.sync.dma_start(n3_t[:], n3)
        nc.sync.dma_start(n4_t[:], n4)
        warm = sbuf("warm", [P, 1], F32)
        nc.scalar.activation(warm[:], half[:], ACT.Abs_reciprocal_sqrt, bias=half[:])
        nc.gpsimd.dma_start(gain[:], gn.rearrange("(p t) o -> p (t o)", t=PACK))

        nc.vector.tensor_copy(xs_pick[:], xs_tab[:].indirect(offs_t[:]))
        nc.vector.tensor_copy(xs_plane[:].bitcast(I32), xs_pick[:].bitcast(I32))
        for j in range(2):
            nc.scalar.dma_start(xs_plane[2 + j : P : 32, :].bitcast(I32), xs_pick[16 + j : P : 32, :].bitcast(I32))
        deal(nc.gpsimd, w1s_deal[:], w1s_raw[:])
        x_pick = sbuf("x_pick", [P, S], U32, tag="xs_tab")
        nc.vector.tensor_copy(x_pick[:, FIRST], x_tab[:].indirect(offs_t[:, FIRST_ENTRIES]))
        w1_by_tile = w1_raw[:].rearrange("p (m t) -> p t m", t=PACK)
        nc.vector.tensor_copy(w1_deal[:, :P], w1_by_tile[:, 0, :])
        nc.vector.tensor_copy(x_pick[:, SECOND], x_tab[:].indirect(offs_t[:, SECOND_ENTRIES]))
        nc.gpsimd.tensor_copy(w1_deal[:, P:].rearrange("p (t m) -> p t m", m=P), w1_by_tile[:, 1:, :])

        w2_raw = sbuf("w2_raw", [P, N], U32, tag="x_tab")
        w2s_raw = sbuf("w2s_raw", [P, N], U8, tag="xs_pick")
        nc.gpsimd.memset(w2s_raw[:].bitcast(I32), 0)
        nc.sync.dma_start(w2_raw[:].bitcast(I32), words_view(w2_words))
        load_scale_rows([nc.sync] * 4, w2s_raw, w2_scales)
        deal(nc.gpsimd, w2_deal[:], w2_raw[:])
        deal(nc.gpsimd, w2s_deal[:], w2s_raw[:])

        def product(name, t, cols, w_deal, ws_deal, codes, scales):
            acc = psum.tile([P, cols.stop - cols.start], F32, name=name, tag="bank_%d_%d" % (t, cols.start))
            rows = slice(t * P, (t + 1) * P)
            nc.tensor.matmul_mx(
                out=acc[:],
                lhsT=w_deal[:, rows].bitcast(FP8X4),
                lhsT_scale=ws_deal[:, rows],
                rhs=codes[:, cols].bitcast(FP8X4),
                rhs_scale=scales[:, cols],
                start=True,
                stop=True,
            )
            return acc

        def products(name, w_deal, ws_deal, codes, scales):
            parts = [[FIRST, SECOND], [ALL], [ALL], [ALL]]
            return [
                [(cols, product("%s%d_%d" % (name, t, cols.start), t, cols, w_deal, ws_deal, codes, scales)) for cols in parts[t]]
                for t in range(PACK)
            ]

        y_n1 = [sbuf("y_n1_%d" % t, [P, S], F32) for t in range(PACK)]
        st = [sbuf("st%d" % t, [P, S], F32) for t in range(PACK)]
        size = [sbuf("size%d" % t, [P, S], F32) for t in range(PACK)]
        root = [sbuf("root%d" % t, [P, S], F32) for t in range(PACK)]
        r_n2 = [sbuf("r_n2_%d" % t, [P, S], F32) for t in range(PACK)]
        z = sbuf("z", [P, PACK, S], F32)
        z_bf = sbuf("z_bf", [P, S, PACK], BF16)
        z_codes = sbuf("z_codes", [P, S], U32)
        z_scales = sbuf("z_scales", [P, S], U8)

        y_acc = products("y_acc", w1_deal, w1s_deal, x_pick, xs_plane)

        def leave_banks(acc, win, t):
            for cols, bank in acc[t]:
                if cols is FIRST:
                    nc.scalar.copy(win[:, cols], bank[:])
                else:
                    nc.vector.tensor_copy(win[:, cols], bank[:])

        def fetch_n1(t):
            for cols, bank in y_acc[t]:
                entries = slice(cols.start // 16, cols.stop // 16)
                nc.scalar.activation(y_n1[t][:, cols], y_win[t][:].indirect(n1_t[:, entries]), ACT.Copy)

        def subtract(t):
            for cols, bank in y_acc[t]:
                nc.vector.tensor_tensor(st[t][:, cols], bank[:], y_n1[t][:, cols], ALU.subtract)

        def size_on_vector(t):
            nc.vector.scalar_tensor_tensor(size[t][:], st[t][:], -1.0, st[t][:], ALU.mult, ALU.max)

        def size_on_scalar(t):
            nc.scalar.activation(size[t][:], st[t][:], ACT.Abs)

        def inverse_root(t):
            nc.scalar.activation(root[t][:], size[t][:], ACT.Abs_reciprocal_sqrt, bias=half[:])

        def ratio(t):
            nc.vector.scalar_tensor_tensor(
                r_win[t][:, :S], root[t][:], gain[:, t : t + 1], root[t][:], ALU.mult, ALU.mult
            )

        def fetch_n2_times_st(t, part):
            cols, entries = HALVES[part]
            nc.vector.tensor_tensor(z[:, t, cols], r_win[t][:].indirect(n2_t[:, entries]), st[t][:, cols], ALU.mult)

        def fetch_n2(t, part):
            cols, entries = HALVES[part]
            nc.scalar.activation(r_n2[t][:, cols], r_win[t][:].indirect(n2_t[:, entries]), ACT.Copy)

        def times_st(t, part):
            cols, entries = HALVES[part]
            nc.vector.tensor_tensor(z[:, t, cols], r_n2[t][:, cols], st[t][:, cols], ALU.mult)

        def quantise(codes, scales, grouped, cols):
            nc.vector.quantize_mx(
                out=codes[:, cols].bitcast(FP8X4),
                scales=scales[:, cols],
                in_=grouped[:, cols, :].rearrange("p s t -> p (s t)"),
            )

        leave_banks(y_acc, y_win[0], 0)
        fetch_n1(0)
        leave_banks(y_acc, y_win[1], 1)
        leave_banks(y_acc, y_win[2], 2)
        fetch_n1(1)
        subtract(0)
        leave_banks(y_acc, y_win[3], 3)
        size_on_vector(0)
        fetch_n1(2)
        subtract(1)
        inverse_root(0)
        size_on_vector(1)
        subtract(2)
        inverse_root(1)
        ratio(0)
        fetch_n1(3)
        ratio(1)
        fetch_n2_times_st(0, 0)
        size_on_scalar(2)
        subtract(3)
        inverse_root(2)
        fetch_n2_times_st(1, 0)
        size_on_scalar(3)
        ratio(2)
        inverse_root(3)
        fetch_n2_times_st(0, 1)
        fetch_n2(2, 0)
        ratio(3)
        fetch_n2_times_st(1, 1)
        fetch_n2(3, 0)
        times_st(2, 0)
        fetch_n2(3, 1)
        times_st(3, 0)
        fetch_n2_times_st(2, 1)
        nc.scalar.copy(z_bf[:, FIRST, :], z[:, :, FIRST].rearrange("p t s -> p s t"))
        times_st(3, 1)
        nc.vector.tensor_copy(z_bf[:, SECOND, :], z[:, :, SECOND].rearrange("p t s -> p s t"))
        quantise(z_codes, z_scales, z_bf, FIRST)
        quantise(z_codes, z_scales, z_bf, SECOND)

        o_bf = sbuf("o_bf", [P, S, PACK], BF16)
        o_codes = sbuf("o_codes", [P, S], U32)
        o_scales = sbuf("o_scales", [P, S], U8)
        o_win = [sbuf("o_win%d" % t, [P, S], F32) for t in range(PACK)]
        old2 = [sbuf("old2_%d" % t, [P, W], F32) for t in range(PACK)]
        ra2 = [sbuf("ra2_%d" % t, [P, W], F32) for t in range(PACK)]
        out_rows = out_0.rearrange("(p t) s -> p t s", t=PACK)
        h_acc = products("h_acc", w2_deal, w2s_deal, z_codes, z_scales)

        def fetch_n3(t):
            nc.scalar.activation(old2[t][:], o_win[t][:].indirect(n3_t[:]), ACT.Copy, scale=-2.0)

        def fetch_n4_plus(t):
            nc.vector.tensor_tensor(ra2[t][:], o_win[t][:].indirect(n4_t[:]), old2[t][:], ALU.add)

        def put_n3(t):
            nc.scalar.activation(o_win[t][:].indirect(n3_t[:]), ra2[t][:], ACT.Copy, scale=-0.5)
            nc.sync.dma_start(out_rows[:, t, :], o_win[t][:])

        def round_plane(t, cols):
            nc.vector.tensor_copy(o_bf[:, cols, t], o_win[t][:, cols])

        for t in range(3):
            leave_banks(h_acc, o_win[t], t)
            fetch_n3(t)
        fetch_n4_plus(0)
        leave_banks(h_acc, o_win[3], 3)
        put_n3(0)
        fetch_n4_plus(1)
        fetch_n3(3)
        fetch_n4_plus(2)
        round_plane(0, ALL)
        fetch_n4_plus(3)
        for t in range(1, 3):
            put_n3(t)
            round_plane(t, ALL)
        put_n3(3)
        round_plane(3, FIRST)
        round_plane(3, SECOND)
        code_words = words_view(out_1)
        for cols in (FIRST, SECOND):
            quantise(o_codes, o_scales, o_bf, cols)
            nc.sync.dma_start(code_words[:, cols], o_codes[:, cols].bitcast(I32))
        scale_rows = out_2[0].bitcast(I32)
        for q in range(4):
            nc.scalar.dma_start(scale_rows[4 * q : 4 * q + 4, :], o_scales[32 * q : 32 * q + 4, :].bitcast(I32))
